import numpy as np
import ml_dtypes


def mxq(x, axis, fmt="e4m3"):
    dtype, down = {"e4m3": (ml_dtypes.float8_e4m3fn, 7), "e5m2": (ml_dtypes.float8_e5m2, 14)}[fmt]
    v = np.moveaxis(np.asarray(x, np.float32).astype(ml_dtypes.bfloat16).astype(np.float64), axis, -1)
    blocks = v.reshape(v.shape[:-1] + (-1, 32))
    amax = np.abs(blocks).max(-1, keepdims=True)
    byte = np.maximum(np.where(amax > 0, np.frexp(amax)[1] - 1 + 127, 0) - down, 1)
    scale = np.exp2(byte - 127.0)
    codes = (blocks / scale).astype(np.float32).astype(dtype).astype(np.float64)
    return np.moveaxis((codes * scale).reshape(v.shape), -1, axis)


WIDE = False


def mx_kscale(k):
    if not WIDE:
        return np.ones(k)
    levels = np.array([10, -10, 5, -5, 0])
    if k % 512:
        return np.exp2(np.random.permutation(np.resize(levels, k // 32))).repeat(32)
    a = np.empty((k // 512, 16))
    for p in range(k // 512):
        a[p, :8] = np.random.permutation(np.resize(levels, 8))
        for g in range(8):
            far = levels[np.abs(levels - a[p, g]) >= 10]
            a[p, g + 8] = far[np.random.randint(len(far))]
    return np.exp2(a.ravel()).repeat(32)


def f64(x):
    return np.asarray(x).astype(np.float64)


def striped(idx):
    return np.tile(idx.reshape(-1, 16).T, (8, 1)).astype(np.uint16)


def unstriped(offs):
    return offs[:16].T.reshape(-1).astype(np.int64)


E2M1 = np.array([0.0, 0.5, 1.0, 1.5, 2.0, 3.0, 4.0, 6.0, -0.0, -0.5, -1.0, -1.5, -2.0, -3.0, -4.0, -6.0])


def pack_weight(w, fmt):
    k, n = w.shape
    w = f64(np.asarray(w, np.float32).astype(ml_dtypes.bfloat16)).reshape(k // 32, 32, n)
    amax = np.abs(w).max(1)
    if fmt == "e4m3":
        byte = np.frexp(amax)[1] - 1 + 127 - 7
    else:
        mant, ex = np.frexp(amax / 6.0)
        byte = np.where(mant > 0.5, ex, ex - 1) + 127
    byte = np.clip(np.where(amax > 0, byte, 1), 1, 254)
    scaled = (w * np.exp2(127.0 - byte)[:, None, :]).reshape(k, n).astype(np.float32)
    by_word = np.ascontiguousarray(scaled.reshape(k // 512, 128, 4, n).transpose(0, 1, 3, 2))
    if fmt == "e4m3":
        words = by_word.astype(ml_dtypes.float8_e4m3fn).view(np.uint8)
    else:
        c = by_word.astype(ml_dtypes.float4_e2m1fn).view(np.uint8) & 0xF
        words = (c[..., 0::2] | (c[..., 1::2] << 4)).reshape(k // 512, 128, 2 * n)
    return np.ascontiguousarray(words), np.ascontiguousarray(byte.astype(np.uint8).reshape(k // 512, 16, n))


def unpack_weight(words, scales, fmt):
    g, _, n = scales.shape
    words = np.ascontiguousarray(words).reshape(g, 128, n, -1)
    if fmt == "e4m3":
        vals = words.view(ml_dtypes.float8_e4m3fn).astype(np.float64)
    else:
        nib = np.empty((g, 128, n, 4), np.uint8)
        nib[..., 0::2] = words & 0xF
        nib[..., 1::2] = words >> 4
        vals = E2M1[nib]
    vals = vals * np.repeat(np.exp2(scales.astype(np.float64) - 127.0), 8, axis=1)[..., None]
    return vals.transpose(0, 1, 3, 2).reshape(g * 512, n)


def gelu(v):
    return 0.5 * v * (1.0 + np.tanh(np.sqrt(2.0 / np.pi) * (v + 0.044715 * v**3)))


def bf(x):
    return np.asarray(x, np.float32).astype(ml_dtypes.bfloat16)


def planes(Y):
    n, m = Y.shape
    b = f64(bf(Y)).reshape(n // 32, 32, m)
    amax = np.abs(b).max(1)
    byte = np.clip(np.where(amax > 0, np.frexp(amax)[1] - 1 + 127 - 7, 1), 1, 254)
    codes = (b * np.exp2(127.0 - byte)[:, None, :]).reshape(n, m).astype(np.float32).astype(ml_dtypes.float8_e4m3fn).view(np.uint8)
    words = codes.reshape(n // 512, 128, 4, m).transpose(0, 1, 3, 2)
    return np.ascontiguousarray(words), np.ascontiguousarray(byte.astype(np.uint8).reshape(n // 512, 16, m))


K, T, S, H, T2, P, N = 1536, 2048, 1024, 512, 2048, 1024, 640


def setup_inputs():
    n = np.random.standard_normal
    s = mx_kscale(K)[:, None]
    u = mx_kscale(H)[:, None]
    d = {}
    d["tab_words"], d["tab_scales"] = pack_weight(n((K, T)) * s, "e4m3")
    d["offs"] = striped(np.random.permutation(T)[:S])
    d["offs2"] = striped(np.random.permutation(T2)[:S])
    d["offs3"] = striped(np.random.permutation(T2)[:P])
    d["w1"] = (1.2 * n((K, H)) / K ** 0.5 / s * u.T).astype(np.float32)
    d["w2_words"], d["w2_scales"] = pack_weight(2.5 * n((K, H)) / K ** 0.5 / s, "e2m1")
    d["gs"] = (2.0 * np.exp(0.3 * n(H)) * u[:, 0]).astype(np.float32)
    d["wgs"] = np.exp(0.3 * n((128, S))).astype(np.float32)
    d["page0"] = (1.5 * n((H, T2)) * u).astype(np.float32)
    d["ginv"] = (1.2 * np.exp(0.3 * n(H)) / u[:, 0]).astype(np.float32)
    d["w3"] = (2.0 * n((H, N)) / H ** 0.5 / u).astype(np.float32)
    return d


def reference(tab_words, tab_scales, offs, offs2, offs3, w1, w2_words, w2_scales, gs, wgs, page0, ginv, w3):
    v = unpack_weight(tab_words, tab_scales, "e4m3")[:, unstriped(offs)]
    w2 = unpack_weight(w2_words, w2_scales, "e2m1")
    a = mxq(f64(w1), 0, "e4m3").T @ v
    b = w2.T @ v
    h = a - f64(gs)[:, None] / (1.0 + np.exp(-b))
    page = f64(page0).copy()
    page[:, unstriped(offs2)] = np.tile(f64(wgs), (H // 128, 1)) * h
    cell = page[:, unstriped(offs3)]
    x = cell / (1.0 + f64(ginv)[:, None] * np.abs(cell))
    y = mxq(f64(w3), 0, "e4m3").T @ mxq(x, 0, "e4m3")
    words, scales = planes(page)
    return y, page, words, scales

@@ -1,0 +1,313 @@
+from contextlib import ExitStack
+
+import concourse.mybir as mybir
+
+K, T, S, H, T2, M_READ, N_OUT = 1536, 2048, 1024, 512, 2048, 1024, 640
+FLOPS = 2 * (2 * K * H * S + H * N_OUT * M_READ)
+
+F32 = mybir.dt.float32
+BF16 = mybir.dt.bfloat16
+I32 = mybir.dt.int32
+U32 = mybir.dt.uint32
+U16 = mybir.dt.uint16
+U8 = mybir.dt.uint8
+FP8X4 = mybir.dt.float8_e4m3fn_x4
+FP4X4 = mybir.dt.float4_e2m1fn_x4
+ACT = mybir.ActivationFunctionType
+ALU = mybir.AluOpType
+
+P = 128
+PACK = 4
+PASSES = K // (P * PACK)
+BANK = 512
+HALVES = S // BANK
+QUAD = 32
+LIST_COLS = BANK // 16
+CHUNKS = T2 // BANK
+
+
+def tile_list_melt_pool_porosity_kernel(
+    tc, tab_words, tab_scales, offs, offs2, offs3, w1, w2_words, w2_scales, gs, wgs, page0, ginv, w3,
+    out_0, out_1, out_2, out_3,
+):
+    nc = tc.nc
+    with ExitStack() as ctx:
+        lists = ctx.enter_context(tc.tile_pool(name="lists", bufs=1))
+        keep = ctx.enter_context(tc.tile_pool(name="keep", bufs=1))
+        psum = ctx.enter_context(tc.psum_pool(name="psum", bufs=1))
+
+        def shared(shape, dtype, name, tag):
+            return keep.tile(shape, dtype, name=name, tag=tag, bufs=1, align_bytes=64)
+
+        def half(h):
+            return slice(h * BANK, (h + 1) * BANK)
+
+        def list_half(tile, h):
+            return tile[:, h * LIST_COLS:(h + 1) * LIST_COLS]
+
+        tab_sc = shared([P, T], U8, "tab_sc", "tab_sc")
+        w2_sc_raw = shared([P, PASSES, H], U8, "w2_sc_raw", "w2_sc_raw")
+        v_sc_low = keep.tile([P, PASSES - 1, S], U8, name="v_sc_low", align_bytes=64)
+        nc.vector.memset(tab_sc[:].bitcast(I32), 0)
+        for q in range(4):
+            nc.scalar.dma_start(
+                out=tab_sc[QUAD * q:QUAD * q + 4 * PASSES, :].bitcast(I32),
+                in_=tab_scales[:, 4 * q:4 * q + 4, :].bitcast(I32),
+            )
+        nc.vector.memset(w2_sc_raw[:].rearrange("p a c -> p (a c)").bitcast(I32), 0)
+        for q in range(4):
+            nc.gpsimd.dma_start(
+                out=w2_sc_raw[QUAD * q:QUAD * q + 4, :, :].bitcast(I32),
+                in_=w2_scales[:, 4 * q:4 * q + 4, :].rearrange("a r c -> r a c").bitcast(I32),
+            )
+        nc.vector.memset(v_sc_low[:].rearrange("p a c -> p (a c)").bitcast(I32), 0)
+        gs_sb = shared([P, PACK], F32, "gs_sb", "gs")
+        nc.scalar.dma_start(out=gs_sb[:], in_=gs.rearrange("(p t) -> p t", t=PACK))
+        neg_gs = keep.tile([P, PACK], F32, name="neg_gs")
+        nc.vector.tensor_scalar(neg_gs[:], gs_sb[:], -1.0, None, ALU.mult)
+
+        w2_raw = shared([P, PASSES, 2 * H], U8, "w2_raw", "w2_raw")
+        nc.sync.dma_start(out=w2_raw[:].bitcast(I32), in_=w2_words.rearrange("a p c -> p a c").bitcast(I32))
+        idx = lists.tile([P, S // 16], U16, name="idx")
+        nc.sync.dma_start(idx[:], offs)
+
+        tab = [None] * PASSES
+        w1_raw = [None] * PASSES
+
+        def load_tab(a, tag):
+            tab[a] = shared([P, T], I32, "tab%d" % a, tag)
+            nc.sync.dma_start(out=tab[a][:], in_=tab_words[a].rearrange("p t i -> p (t i)").bitcast(I32))
+
+        def load_w1(a, tag):
+            w1_raw[a] = shared([P, PACK, H], F32, "w1_raw%d" % a, tag)
+            rows = w1[a * P * PACK:(a + 1) * P * PACK, :]
+            nc.sync.dma_start(out=w1_raw[a][:], in_=rows.rearrange("(p j) c -> p j c", j=PACK))
+
+        load_tab(0, "tab0")
+        load_tab(1, "tab1")
+        load_w1(0, "gs")
+
+        page_rows = page0.rearrange("(p t) c -> t p c", t=PACK)
+        out_rows = out_1.rearrange("(p t) c -> t p c", t=PACK)
+        page = [None] * PACK
+
+        def load_page(t, tag):
+            page[t] = shared([P, T2], F32, "page%d" % t, tag)
+            nc.sync.dma_start(out=page[t][:], in_=page_rows[t])
+
+        idx2 = lists.tile([P, S // 16], U16, name="idx2")
+        nc.sync.dma_start(idx2[:], offs2)
+        idx3 = lists.tile([P, M_READ // 16], U16, name="idx3")
+        nc.sync.dma_start(idx3[:], offs3)
+
+        w2_dealt = shared([P, PASSES, 2 * H], U8, "w2_dealt", "w2_dealt")
+        nc.vector.tensor_copy(
+            out=w2_dealt[:].bitcast(U16).rearrange("p a (t m) -> p a t m", t=PACK),
+            in_=w2_raw[:].bitcast(U16).rearrange("p a (m t) -> p a t m", t=PACK),
+        )
+        load_tab(2, "w2_raw")
+        v_words = [keep.tile([P, S], U32, name="v_words%d" % a, align_bytes=64) for a in range(PASSES)]
+        v_sc = keep.tile([P, S], U8, name="v_sc", align_bytes=64)
+
+        def gather_words(a):
+            nc.vector.tensor_copy(v_words[a][:], tab[a][:].bitcast(U32).indirect(idx[:]))
+
+        gather_words(0)
+        load_w1(1, "tab0")
+        nc.vector.tensor_copy(v_sc[:], tab_sc[:].indirect(idx[:]))
+        moved = 112
+        for a in range(1, PASSES):
+            nc.sync.dma_start(
+                out=v_sc_low[0:moved, a - 1, :].bitcast(I32),
+                in_=v_sc[4 * a:4 * a + moved, :].bitcast(I32),
+            )
+
+        wgs_rows = wgs.rearrange("(q t) j -> q t j", t=PACK)
+        load_w1(2, "tab_sc")
+
+        gather_words(1)
+        load_page(0, "tab1")
+        w2_sc = keep.tile([P, PASSES, H], U8, name="w2_sc", align_bytes=64)
+        nc.gpsimd.tensor_copy(
+            out=w2_sc[:].rearrange("p a (t m) -> p a t m", t=PACK),
+            in_=w2_sc_raw[:].rearrange("p a (m t) -> p a t m", t=PACK),
+        )
+        ginv_sb = shared([P, PACK], F32, "ginv_sb", "w2_sc_raw")
+        nc.sync.dma_start(out=ginv_sb[:], in_=ginv.rearrange("(p t) -> p t", t=PACK))
+        gather_words(2)
+        wg_first = shared([P, S], F32, "wg_first", "w2_raw")
+        for q in (0, 2, 1, 3):
+            nc.sync.dma_start(out=wg_first[QUAD * q:QUAD * (q + 1), :], in_=wgs_rows[:, 0, :])
+
+        w1_codes = [keep.tile([P, H], U32, name="w1_codes%d" % a, align_bytes=64) for a in range(PASSES)]
+        w1_sc = [keep.tile([P, H], U8, name="w1_sc%d" % a, align_bytes=64) for a in range(PASSES)]
+        for a in range(PASSES):
+            w1_bf = shared([P, PACK * H], BF16, "w1_bf%d" % a, "w1_bf%d" % a)
+            dst = w1_bf[:].rearrange("p (t m j) -> p m j t", t=PACK, j=PACK)
+            src = w1_raw[a][:].rearrange("p j (m t) -> p m j t", t=PACK)
+            if a < PASSES - 1:
+                nc.scalar.copy(out=dst, in_=src)
+            else:
+                nc.vector.tensor_copy(out=dst, in_=src)
+            nc.vector.quantize_mx(out=w1_codes[a][:].bitcast(FP8X4), scales=w1_sc[a][:], in_=w1_bf[:])
+        load_page(1, "tab_sc")
+        wg_rest = shared([P, PACK - 1, S], F32, "wg_rest", "w1_bf1")
+        for q in (0, 2, 1, 3):
+            nc.sync.dma_start(out=wg_rest[QUAD * q:QUAD * (q + 1), :, :], in_=wgs_rows[:, 1:PACK, :])
+
+        hs = [shared([P, S], F32, "h%d" % t, "tab0" if t == 0 else "h%d" % t) for t in range(PACK)]
+
+        def sigmoid_b(t):
+            for h in range(HALVES):
+                acc = psum.tile([P, BANK], F32, name="b_sum", tag="left%d" % h if t == 0 else "right%d" % h)
+                for a in range(PASSES):
+                    v_plane = v_sc[:, half(h)] if a == 0 else v_sc_low[:, a - 1, half(h)]
+                    nc.tensor.matmul_mx(
+                        out=acc[:],
+                        lhsT=w2_dealt[:, a, 2 * P * t:2 * P * (t + 1)].bitcast(FP4X4),
+                        lhsT_scale=w2_sc[:, a, P * t:P * (t + 1)],
+                        rhs=v_words[a][:, half(h)].bitcast(FP8X4),
+                        rhs_scale=v_plane,
+                        start=(a == 0), stop=(a == PASSES - 1),
+                    )
+                nc.scalar.activation(hs[t][:, half(h)], acc[:], ACT.Sigmoid)
+
+        def make_h(t):
+            for h in range(HALVES):
+                acc = psum.tile([P, BANK], F32, name="a_sum", tag="left%d" % h if t % 2 else "right%d" % h)
+                for a in range(PASSES):
+                    nc.tensor.matmul_mx(
+                        out=acc[:],
+                        lhsT=w1_codes[a][:, P * t:P * (t + 1)].bitcast(FP8X4),
+                        lhsT_scale=w1_sc[a][:, P * t:P * (t + 1)],
+                        rhs=v_words[a][:, half(h)].bitcast(FP8X4),
+                        rhs_scale=v_sc[4 * a:P, half(h)],
+                        start=(a == 0), stop=(a == PASSES - 1),
+                    )
+                nc.vector.scalar_tensor_tensor(
+                    hs[t][:, half(h)], hs[t][:, half(h)], neg_gs[:, t:t + 1], acc[:], ALU.mult, ALU.add
+                )
+
+        def scatter(t):
+            if t == 0:
+                for h in range(HALVES):
+                    nc.vector.tensor_tensor(
+                        page[t][:].indirect(list_half(idx2, h)), hs[t][:, half(h)], wg_first[:, half(h)], ALU.mult
+                    )
+            else:
+                nc.vector.tensor_tensor(page[t][:].indirect(idx2[:]), hs[t][:], wg_rest[:, t - 1, :], ALU.mult)
+            nc.sync.dma_start(out=out_rows[t], in_=page[t][:])
+
+        cells = [shared([P, PACK, BANK], F32, "cells%d" % h, "cells%d" % h) for h in range(HALVES)]
+        gain = [shared([P, PACK, BANK], F32, "gain%d" % h, "gain%d" % h) for h in range(HALVES)]
+        pairs = [keep.tile([P, 2, T2 // 2, 2], BF16, name="pairs%d" % c) for c in range(2)]
+
+        def read_cells(t, width):
+            pieces = [(lo // BANK, slice(lo % BANK, lo % BANK + width), slice(lo // 16, (lo + width) // 16))
+                      for lo in range(0, M_READ, width)]
+            for h, cols, entries in pieces:
+                nc.vector.tensor_copy(cells[h][:, t, cols], page[t][:].indirect(idx3[:, entries]))
+            for first in range(0, len(pieces), 2):
+                for h, cols, entries in pieces[first:first + 2]:
+                    nc.scalar.activation(gain[h][:, t, cols], cells[h][:, t, cols], ACT.Abs, scale=ginv_sb[:, t:t + 1])
+                for h, cols, entries in pieces[first:first + 2]:
+                    nc.scalar.activation(gain[h][:, t, cols], gain[h][:, t, cols], ACT.Abs_reciprocal_sqrt, bias=1.0)
+                for h, cols, entries in pieces[first:first + 2]:
+                    nc.scalar.activation(gain[h][:, t, cols], gain[h][:, t, cols], ACT.Square)
+
+        def round_page(t, width):
+            for lo in range(0, T2, width):
+                c, at = divmod(lo, T2 // 2)
+                nc.scalar.copy(out=pairs[c][:, t // 2, at:at + width, t % 2], in_=page[t][:, lo:lo + width])
+
+        w3_codes = keep.tile([P, N_OUT], U32, name="w3_codes", align_bytes=64)
+        w3_sc = keep.tile([P, N_OUT], U8, name="w3_sc", align_bytes=64)
+
+        def quantise_w3():
+            w3_bf = shared([P, PACK * N_OUT], BF16, "w3_bf", "gs")
+            nc.scalar.copy(
+                out=w3_bf[:].rearrange("p (c i j) -> p c j i", i=4, j=PACK),
+                in_=w3_raw[:].rearrange("p j (c i) -> p c j i", i=4),
+            )
+            for lo, hi in ((0, BANK), (BANK, N_OUT)):
+                nc.vector.quantize_mx(
+                    out=w3_codes[:, lo:hi].bitcast(FP8X4), scales=w3_sc[:, lo:hi], in_=w3_bf[:, PACK * lo:PACK * hi]
+                )
+
+        sigmoid_b(0)
+        make_h(0)
+        sigmoid_b(1)
+        scatter(0)
+        load_page(2, "w2_raw")
+        load_page(3, "tab0")
+        sigmoid_b(2)
+        make_h(1)
+        sigmoid_b(3)
+        w3_raw = shared([P, PACK, N_OUT], F32, "w3_raw", "w2_dealt")
+        nc.sync.dma_start(out=w3_raw[:], in_=w3.rearrange("(p j) n -> p j n", j=PACK))
+        for t in range(1, PACK):
+            read_cells(t - 1, BANK)
+            scatter(t)
+            round_page(t - 1, T2 // 2)
+            if t + 1 < PACK:
+                make_h(t + 1)
+            if t == 2:
+                quantise_w3()
+        read_cells(PACK - 1, BANK // 2)
+
+        x_codes = keep.tile([P, M_READ], U32, name="x_codes", align_bytes=64)
+        x_sc = keep.tile([P, M_READ], U8, name="x_sc", align_bytes=64)
+        x_bf = [shared([P, PACK * BANK], BF16, "x_bf%d" % h, "w1_bf%d" % (2 * h)) for h in range(HALVES)]
+        y_rows = out_0.rearrange("(b p) m -> b p m", p=P)
+
+        def weave_x(h):
+            nc.vector.tensor_tensor(
+                x_bf[h][:].rearrange("p (c i t) -> p c t i", i=4, t=PACK),
+                cells[h][:].rearrange("p t (c i) -> p c t i", i=4),
+                gain[h][:].rearrange("p t (c i) -> p c t i", i=4),
+                ALU.mult,
+            )
+
+        def rate(h):
+            nc.vector.quantize_mx(out=x_codes[:, half(h)].bitcast(FP8X4), scales=x_sc[:, half(h)], in_=x_bf[h][:])
+            for b in range(N_OUT // P):
+                acc = psum.tile([P, BANK], F32, name="y_sum", bufs=4)
+                nc.tensor.matmul_mx(
+                    out=acc[:],
+                    lhsT=w3_codes[:, P * b:P * (b + 1)].bitcast(FP8X4),
+                    lhsT_scale=w3_sc[:, P * b:P * (b + 1)],
+                    rhs=x_codes[:, half(h)].bitcast(FP8X4),
+                    rhs_scale=x_sc[:, half(h)],
+                    start=True, stop=True,
+                )
+                y_sb = keep.tile([P, BANK], F32, name="y_sb", bufs=2 * (N_OUT // P))
+                nc.scalar.copy(out=y_sb[:], in_=acc[:])
+                nc.sync.dma_start(out=y_rows[b][:, half(h)], in_=y_sb[:])
+
+        weave_x(0)
+        round_page(PACK - 1, BANK)
+        rate(0)
+        weave_x(1)
+        rate(1)
+
+        page_codes = keep.tile([P, T2], U32, name="page_codes", align_bytes=64)
+        page_sc = keep.tile([P, T2], U8, name="page_sc", align_bytes=64)
+        words_out = out_2[0].rearrange("p m t -> p (m t)").bitcast(I32)
+        page_bf = []
+        for c in range(CHUNKS + 1):
+            if c < CHUNKS:
+                page_bf.append(shared([P, PACK * BANK], BF16, "page_bf%d" % c, ("gain1", "cells1")[c % 2]))
+                words = pairs[c // 2][:].rearrange("p u m e -> p u (m e)").bitcast(I32)
+                nc.vector.tensor_copy(
+                    out=page_bf[c][:].bitcast(I32).rearrange("p (m u) -> p m u", u=2),
+                    in_=words[:, :, half(c % 2)].rearrange("p u m -> p m u"),
+                )
+            if c > 0:
+                cols = half(c - 1)
+                nc.vector.quantize_mx(out=page_codes[:, cols].bitcast(FP8X4), scales=page_sc[:, cols], in_=page_bf[c - 1][:])
+                nc.sync.dma_start(out=words_out[:, cols], in_=page_codes[:, cols].bitcast(I32))
+        for q in range(4):
+            nc.scalar.dma_start(
+                out=out_3[0, 4 * q:4 * q + 4, :].bitcast(I32),
+                in_=page_sc[QUAD * q:QUAD * q + 4, :].bitcast(I32),
+            )

@@ -45,99 +45,98 @@ def tile_list_melt_pool_porosity_kernel(
         def list_half(tile, h):
             return tile[:, h * LIST_COLS:(h + 1) * LIST_COLS]
 
-        tab_sc = shared([P, T], U8, "tab_sc", "tab_sc")
-        w2_sc_raw = shared([P, PASSES, H], U8, "w2_sc_raw", "w2_sc_raw")
+        w2_sc_raw = keep.tile([P, PASSES, H], U8, name="w2_sc_raw", align_bytes=64)
+        tab_sc = keep.tile([P, T], U8, name="tab_sc", align_bytes=64)
         v_sc_low = keep.tile([P, PASSES - 1, S], U8, name="v_sc_low", align_bytes=64)
         nc.vector.memset(tab_sc[:].bitcast(I32), 0)
+        nc.vector.memset(w2_sc_raw[:].rearrange("p a c -> p (a c)").bitcast(I32), 0)
+        nc.vector.memset(v_sc_low[:].rearrange("p a c -> p (a c)").bitcast(I32), 0)
         for q in range(4):
             nc.scalar.dma_start(
                 out=tab_sc[QUAD * q:QUAD * q + 4 * PASSES, :].bitcast(I32),
                 in_=tab_scales[:, 4 * q:4 * q + 4, :].bitcast(I32),
             )
-        nc.vector.memset(w2_sc_raw[:].rearrange("p a c -> p (a c)").bitcast(I32), 0)
         for q in range(4):
-            nc.gpsimd.dma_start(
+            nc.scalar.dma_start(
                 out=w2_sc_raw[QUAD * q:QUAD * q + 4, :, :].bitcast(I32),
                 in_=w2_scales[:, 4 * q:4 * q + 4, :].rearrange("a r c -> r a c").bitcast(I32),
             )
-        nc.vector.memset(v_sc_low[:].rearrange("p a c -> p (a c)").bitcast(I32), 0)
-        gs_sb = shared([P, PACK], F32, "gs_sb", "gs")
-        nc.scalar.dma_start(out=gs_sb[:], in_=gs.rearrange("(p t) -> p t", t=PACK))
-        neg_gs = keep.tile([P, PACK], F32, name="neg_gs")
-        nc.vector.tensor_scalar(neg_gs[:], gs_sb[:], -1.0, None, ALU.mult)
 
-        w2_raw = shared([P, PASSES, 2 * H], U8, "w2_raw", "w2_raw")
+        w2_raw = keep.tile([P, PASSES, 2 * H], U8, name="w2_raw", align_bytes=64)
         nc.sync.dma_start(out=w2_raw[:].bitcast(I32), in_=w2_words.rearrange("a p c -> p a c").bitcast(I32))
         idx = lists.tile([P, S // 16], U16, name="idx")
         nc.sync.dma_start(idx[:], offs)
+        idx2 = lists.tile([P, S // 16], U16, name="idx2")
+        nc.sync.dma_start(idx2[:], offs2)
 
-        tab = [None] * PASSES
-        w1_raw = [None] * PASSES
+        tab = [shared([P, T], I32, "tab%d" % a, "tab%d" % a) for a in range(PASSES)]
+        w1_raw = [shared([P, PACK, H], F32, "w1_raw%d" % a, "w1_raw%d" % a) for a in range(PASSES)]
 
-        def load_tab(a, tag):
-            tab[a] = shared([P, T], I32, "tab%d" % a, tag)
+        def load_tab(a):
             nc.sync.dma_start(out=tab[a][:], in_=tab_words[a].rearrange("p t i -> p (t i)").bitcast(I32))
 
-        def load_w1(a, tag):
-            w1_raw[a] = shared([P, PACK, H], F32, "w1_raw%d" % a, tag)
+        def load_w1(a):
             rows = w1[a * P * PACK:(a + 1) * P * PACK, :]
             nc.sync.dma_start(out=w1_raw[a][:], in_=rows.rearrange("(p j) c -> p j c", j=PACK))
 
-        load_tab(0, "tab0")
-        load_tab(1, "tab1")
-        load_w1(0, "gs")
+        load_tab(0)
+        load_tab(1)
+        load_w1(0)
+        load_tab(2)
+        load_w1(1)
+        load_w1(2)
+        gs_sb = keep.tile([P, PACK], F32, name="gs_sb")
+        nc.sync.dma_start(out=gs_sb[:], in_=gs.rearrange("(p t) -> p t", t=PACK))
 
-        page_rows = page0.rearrange("(p t) c -> t p c", t=PACK)
-        out_rows = out_1.rearrange("(p t) c -> t p c", t=PACK)
-        page = [None] * PACK
-
-        def load_page(t, tag):
-            page[t] = shared([P, T2], F32, "page%d" % t, tag)
-            nc.sync.dma_start(out=page[t][:], in_=page_rows[t])
-
-        idx2 = lists.tile([P, S // 16], U16, name="idx2")
-        nc.sync.dma_start(idx2[:], offs2)
-        idx3 = lists.tile([P, M_READ // 16], U16, name="idx3")
-        nc.sync.dma_start(idx3[:], offs3)
-
-        w2_dealt = shared([P, PASSES, 2 * H], U8, "w2_dealt", "w2_dealt")
+        w2_dealt = keep.tile([P, PASSES, 2 * H], U8, name="w2_dealt", align_bytes=64)
         nc.vector.tensor_copy(
             out=w2_dealt[:].bitcast(U16).rearrange("p a (t m) -> p a t m", t=PACK),
             in_=w2_raw[:].bitcast(U16).rearrange("p a (m t) -> p a t m", t=PACK),
         )
-        load_tab(2, "w2_raw")
         v_words = [keep.tile([P, S], U32, name="v_words%d" % a, align_bytes=64) for a in range(PASSES)]
         v_sc = keep.tile([P, S], U8, name="v_sc", align_bytes=64)
 
         def gather_words(a):
             nc.vector.tensor_copy(v_words[a][:], tab[a][:].bitcast(U32).indirect(idx[:]))
 
-        gather_words(0)
-        load_w1(1, "tab0")
         nc.vector.tensor_copy(v_sc[:], tab_sc[:].indirect(idx[:]))
         moved = 112
         for a in range(1, PASSES):
-            nc.sync.dma_start(
+            nc.scalar.dma_start(
                 out=v_sc_low[0:moved, a - 1, :].bitcast(I32),
                 in_=v_sc[4 * a:4 * a + moved, :].bitcast(I32),
             )
-
-        wgs_rows = wgs.rearrange("(q t) j -> q t j", t=PACK)
-        load_w1(2, "tab_sc")
-
-        gather_words(1)
-        load_page(0, "tab1")
+        gather_words(0)
         w2_sc = keep.tile([P, PASSES, H], U8, name="w2_sc", align_bytes=64)
-        nc.gpsimd.tensor_copy(
+        nc.vector.tensor_copy(
             out=w2_sc[:].rearrange("p a (t m) -> p a t m", t=PACK),
             in_=w2_sc_raw[:].rearrange("p a (m t) -> p a t m", t=PACK),
         )
-        ginv_sb = shared([P, PACK], F32, "ginv_sb", "w2_sc_raw")
-        nc.sync.dma_start(out=ginv_sb[:], in_=ginv.rearrange("(p t) -> p t", t=PACK))
+        gather_words(1)
         gather_words(2)
-        wg_first = shared([P, S], F32, "wg_first", "w2_raw")
+        neg_gs = keep.tile([P, PACK], F32, name="neg_gs")
+        nc.vector.tensor_scalar(neg_gs[:], gs_sb[:], -1.0, None, ALU.mult)
+
+        page_rows = page0.rearrange("(p t) c -> t p c", t=PACK)
+        out_rows = out_1.rearrange("(p t) c -> t p c", t=PACK)
+        wgs_rows = wgs.rearrange("(q t) j -> q t j", t=PACK)
+        page = [keep.tile([P, T2], F32, name="page%d" % t) for t in range(PACK)]
+        idx3 = lists.tile([P, M_READ // 16], U16, name="idx3")
+        wg_first = keep.tile([P, S], F32, name="wg_first")
+        wg_rest = keep.tile([P, PACK - 1, S], F32, name="wg_rest")
+        ginv_sb = keep.tile([P, PACK], F32, name="ginv_sb")
+        w3_raw = keep.tile([P, PACK, N_OUT], F32, name="w3_raw")
+        nc.sync.dma_start(out=page[0][:], in_=page_rows[0])
         for q in (0, 2, 1, 3):
             nc.sync.dma_start(out=wg_first[QUAD * q:QUAD * (q + 1), :], in_=wgs_rows[:, 0, :])
+        nc.sync.dma_start(idx3[:], offs3)
+        nc.sync.dma_start(out=ginv_sb[:], in_=ginv.rearrange("(p t) -> p t", t=PACK))
+        nc.sync.dma_start(out=page[1][:], in_=page_rows[1])
+        for q in (0, 2, 1, 3):
+            nc.sync.dma_start(out=wg_rest[QUAD * q:QUAD * (q + 1), :, :], in_=wgs_rows[:, 1:PACK, :])
+        nc.sync.dma_start(out=page[2][:], in_=page_rows[2])
+        nc.sync.dma_start(out=w3_raw[:], in_=w3.rearrange("(p j) n -> p j n", j=PACK))
+        nc.sync.dma_start(out=page[3][:], in_=page_rows[3])
 
         w1_codes = [keep.tile([P, H], U32, name="w1_codes%d" % a, align_bytes=64) for a in range(PASSES)]
         w1_sc = [keep.tile([P, H], U8, name="w1_sc%d" % a, align_bytes=64) for a in range(PASSES)]
@@ -150,12 +149,8 @@ def tile_list_melt_pool_porosity_kernel(
             else:
                 nc.vector.tensor_copy(out=dst, in_=src)
             nc.vector.quantize_mx(out=w1_codes[a][:].bitcast(FP8X4), scales=w1_sc[a][:], in_=w1_bf[:])
-        load_page(1, "tab_sc")
-        wg_rest = shared([P, PACK - 1, S], F32, "wg_rest", "w1_bf1")
-        for q in (0, 2, 1, 3):
-            nc.sync.dma_start(out=wg_rest[QUAD * q:QUAD * (q + 1), :, :], in_=wgs_rows[:, 1:PACK, :])
 
-        hs = [shared([P, S], F32, "h%d" % t, "tab0" if t == 0 else "h%d" % t) for t in range(PACK)]
+        hs = [shared([P, S], F32, "h%d" % t, "w1_raw1" if t == 0 else "h%d" % t) for t in range(PACK)]
 
         def sigmoid_b(t):
             for h in range(HALVES):
@@ -198,9 +193,8 @@ def tile_list_melt_pool_porosity_kernel(
                 nc.vector.tensor_tensor(page[t][:].indirect(idx2[:]), hs[t][:], wg_rest[:, t - 1, :], ALU.mult)
             nc.sync.dma_start(out=out_rows[t], in_=page[t][:])
 
-        cells = [shared([P, PACK, BANK], F32, "cells%d" % h, "cells%d" % h) for h in range(HALVES)]
-        gain = [shared([P, PACK, BANK], F32, "gain%d" % h, "gain%d" % h) for h in range(HALVES)]
-        pairs = [keep.tile([P, 2, T2 // 2, 2], BF16, name="pairs%d" % c) for c in range(2)]
+        cells = [shared([P, PACK, BANK], F32, "cells%d" % h, "tab%d" % h) for h in range(HALVES)]
+        gain = [shared([P, PACK, BANK], F32, "gain%d" % h, ("tab2", "w1_raw0")[h]) for h in range(HALVES)]
 
         def read_cells(t, width):
             pieces = [(lo // BANK, slice(lo % BANK, lo % BANK + width), slice(lo // 16, (lo + width) // 16))
@@ -224,7 +218,7 @@ def tile_list_melt_pool_porosity_kernel(
         w3_sc = keep.tile([P, N_OUT], U8, name="w3_sc", align_bytes=64)
 
         def quantise_w3():
-            w3_bf = shared([P, PACK * N_OUT], BF16, "w3_bf", "gs")
+            w3_bf = shared([P, PACK * N_OUT], BF16, "w3_bf", "w1_bf0")
             nc.scalar.copy(
                 out=w3_bf[:].rearrange("p (c i j) -> p c j i", i=4, j=PACK),
                 in_=w3_raw[:].rearrange("p j (c i) -> p c j i", i=4),
@@ -238,13 +232,10 @@ def tile_list_melt_pool_porosity_kernel(
         make_h(0)
         sigmoid_b(1)
         scatter(0)
-        load_page(2, "w2_raw")
-        load_page(3, "tab0")
+        pairs = [shared([P, 2, T2 // 2, 2], BF16, "pairs%d" % c, "w1_raw%d" % (c + 1)) for c in range(2)]
         sigmoid_b(2)
         make_h(1)
         sigmoid_b(3)
-        w3_raw = shared([P, PACK, N_OUT], F32, "w3_raw", "w2_dealt")
-        nc.sync.dma_start(out=w3_raw[:], in_=w3.rearrange("(p j) n -> p j n", j=PACK))
         for t in range(1, PACK):
             read_cells(t - 1, BANK)
             scatter(t)
@@ -257,10 +248,11 @@ def tile_list_melt_pool_porosity_kernel(
 
         x_codes = keep.tile([P, M_READ], U32, name="x_codes", align_bytes=64)
         x_sc = keep.tile([P, M_READ], U8, name="x_sc", align_bytes=64)
-        x_bf = [shared([P, PACK * BANK], BF16, "x_bf%d" % h, "w1_bf%d" % (2 * h)) for h in range(HALVES)]
+        x_bf = [None] * HALVES
         y_rows = out_0.rearrange("(b p) m -> b p m", p=P)
 
         def weave_x(h):
+            x_bf[h] = shared([P, PACK * BANK], BF16, "x_bf%d" % h, "w1_bf1")
             nc.vector.tensor_tensor(
                 x_bf[h][:].rearrange("p (c i t) -> p c t i", i=4, t=PACK),
                 cells[h][:].rearrange("p t (c i) -> p c t i", i=4),
@@ -296,7 +288,7 @@ def tile_list_melt_pool_porosity_kernel(
         page_bf = []
         for c in range(CHUNKS + 1):
             if c < CHUNKS:
-                page_bf.append(shared([P, PACK * BANK], BF16, "page_bf%d" % c, ("gain1", "cells1")[c % 2]))
+                page_bf.append(shared([P, PACK * BANK], BF16, "page_bf%d" % c, ("w1_raw0", "tab1")[c % 2]))
                 words = pairs[c // 2][:].rearrange("p u m e -> p u (m e)").bitcast(I32)
                 nc.vector.tensor_copy(
                     out=page_bf[c][:].bitcast(I32).rearrange("p (m u) -> p m u", u=2),

@@ -66,8 +66,6 @@ def tile_list_melt_pool_porosity_kernel(
         nc.sync.dma_start(out=w2_raw[:].bitcast(I32), in_=w2_words.rearrange("a p c -> p a c").bitcast(I32))
         idx = lists.tile([P, S // 16], U16, name="idx")
         nc.sync.dma_start(idx[:], offs)
-        idx2 = lists.tile([P, S // 16], U16, name="idx2")
-        nc.sync.dma_start(idx2[:], offs2)
 
         tab = [shared([P, T], I32, "tab%d" % a, "tab%d" % a) for a in range(PASSES)]
         w1_raw = [shared([P, PACK, H], F32, "w1_raw%d" % a, "w1_raw%d" % a) for a in range(PASSES)]
@@ -79,12 +77,9 @@ def tile_list_melt_pool_porosity_kernel(
             rows = w1[a * P * PACK:(a + 1) * P * PACK, :]
             nc.sync.dma_start(out=w1_raw[a][:], in_=rows.rearrange("(p j) c -> p j c", j=PACK))
 
-        load_tab(0)
-        load_tab(1)
-        load_w1(0)
-        load_tab(2)
-        load_w1(1)
-        load_w1(2)
+        for a in range(PASSES):
+            load_tab(a)
+            load_w1(a)
         gs_sb = keep.tile([P, PACK], F32, name="gs_sb")
         nc.sync.dma_start(out=gs_sb[:], in_=gs.rearrange("(p t) -> p t", t=PACK))
 
@@ -121,12 +116,14 @@ def tile_list_melt_pool_porosity_kernel(
         out_rows = out_1.rearrange("(p t) c -> t p c", t=PACK)
         wgs_rows = wgs.rearrange("(q t) j -> q t j", t=PACK)
         page = [keep.tile([P, T2], F32, name="page%d" % t) for t in range(PACK)]
+        idx2 = lists.tile([P, S // 16], U16, name="idx2")
         idx3 = lists.tile([P, M_READ // 16], U16, name="idx3")
         wg_first = keep.tile([P, S], F32, name="wg_first")
         wg_rest = keep.tile([P, PACK - 1, S], F32, name="wg_rest")
         ginv_sb = keep.tile([P, PACK], F32, name="ginv_sb")
         w3_raw = keep.tile([P, PACK, N_OUT], F32, name="w3_raw")
         nc.sync.dma_start(out=page[0][:], in_=page_rows[0])
+        nc.sync.dma_start(idx2[:], offs2)
         for q in (0, 2, 1, 3):
             nc.sync.dma_start(out=wg_first[QUAD * q:QUAD * (q + 1), :], in_=wgs_rows[:, 0, :])
         nc.sync.dma_start(idx3[:], offs3)
@@ -148,13 +145,18 @@ def tile_list_melt_pool_porosity_kernel(
                 nc.scalar.copy(out=dst, in_=src)
             else:
                 nc.vector.tensor_copy(out=dst, in_=src)
-            nc.vector.quantize_mx(out=w1_codes[a][:].bitcast(FP8X4), scales=w1_sc[a][:], in_=w1_bf[:])
+            cuts = (0, H) if a < PASSES - 1 else (0, P, 2 * P, H)
+            for lo, hi in zip(cuts, cuts[1:]):
+                nc.vector.quantize_mx(
+                    out=w1_codes[a][:, lo:hi].bitcast(FP8X4), scales=w1_sc[a][:, lo:hi], in_=w1_bf[:, PACK * lo:PACK * hi]
+                )
 
-        hs = [shared([P, S], F32, "h%d" % t, "w1_raw1" if t == 0 else "h%d" % t) for t in range(PACK)]
+        sig = [keep.tile([P, S], F32, name="sig%d" % t) for t in range(PACK)]
+        hs = [None] * PACK
 
         def sigmoid_b(t):
             for h in range(HALVES):
-                acc = psum.tile([P, BANK], F32, name="b_sum", tag="left%d" % h if t == 0 else "right%d" % h)
+                acc = psum.tile([P, BANK], F32, name="b_sum", tag="bank%d" % (h if t == 0 else 2 + h))
                 for a in range(PASSES):
                     v_plane = v_sc[:, half(h)] if a == 0 else v_sc_low[:, a - 1, half(h)]
                     nc.tensor.matmul_mx(
@@ -165,22 +167,25 @@ def tile_list_melt_pool_porosity_kernel(
                         rhs_scale=v_plane,
                         start=(a == 0), stop=(a == PASSES - 1),
                     )
-                nc.scalar.activation(hs[t][:, half(h)], acc[:], ACT.Sigmoid)
+                nc.scalar.activation(sig[t][:, half(h)], acc[:], ACT.Sigmoid)
 
         def make_h(t):
-            for h in range(HALVES):
-                acc = psum.tile([P, BANK], F32, name="a_sum", tag="left%d" % h if t % 2 else "right%d" % h)
+            width = BANK // 2 if t == 0 else BANK
+            hs[t] = shared([P, S], F32, "h%d" % t, "h")
+            for n, lo in enumerate(range(0, S, width)):
+                cols = slice(lo, lo + width)
+                acc = psum.tile([P, width], F32, name="a_sum", tag="bank%d" % (2 + 2 * (t % 2) + n))
                 for a in range(PASSES):
                     nc.tensor.matmul_mx(
                         out=acc[:],
                         lhsT=w1_codes[a][:, P * t:P * (t + 1)].bitcast(FP8X4),
                         lhsT_scale=w1_sc[a][:, P * t:P * (t + 1)],
-                        rhs=v_words[a][:, half(h)].bitcast(FP8X4),
-                        rhs_scale=v_sc[4 * a:P, half(h)],
+                        rhs=v_words[a][:, cols].bitcast(FP8X4),
+                        rhs_scale=v_sc[4 * a:P, cols],
                         start=(a == 0), stop=(a == PASSES - 1),
                     )
                 nc.vector.scalar_tensor_tensor(
-                    hs[t][:, half(h)], hs[t][:, half(h)], neg_gs[:, t:t + 1], acc[:], ALU.mult, ALU.add
+                    hs[t][:, cols], sig[t][:, cols], neg_gs[:, t:t + 1], acc[:], ALU.mult, ALU.add
                 )
 
         def scatter(t):
@@ -263,7 +268,7 @@ def tile_list_melt_pool_porosity_kernel(
         def rate(h):
             nc.vector.quantize_mx(out=x_codes[:, half(h)].bitcast(FP8X4), scales=x_sc[:, half(h)], in_=x_bf[h][:])
             for b in range(N_OUT // P):
-                acc = psum.tile([P, BANK], F32, name="y_sum", bufs=4)
+                acc = psum.tile([P, BANK], F32, name="y_sum", tag="bank%d" % ((h * (N_OUT // P) + b) % 8))
                 nc.tensor.matmul_mx(
                     out=acc[:],
                     lhsT=w3_codes[:, P * b:P * (b + 1)].bitcast(FP8X4),
@@ -276,28 +281,34 @@ def tile_list_melt_pool_porosity_kernel(
                 nc.scalar.copy(out=y_sb[:], in_=acc[:])
                 nc.sync.dma_start(out=y_rows[b][:, half(h)], in_=y_sb[:])
 
-        weave_x(0)
-        round_page(PACK - 1, BANK)
-        rate(0)
-        weave_x(1)
-        rate(1)
-
         page_codes = keep.tile([P, T2], U32, name="page_codes", align_bytes=64)
         page_sc = keep.tile([P, T2], U8, name="page_sc", align_bytes=64)
         words_out = out_2[0].rearrange("p m t -> p (m t)").bitcast(I32)
-        page_bf = []
-        for c in range(CHUNKS + 1):
-            if c < CHUNKS:
-                page_bf.append(shared([P, PACK * BANK], BF16, "page_bf%d" % c, ("w1_raw0", "tab1")[c % 2]))
-                words = pairs[c // 2][:].rearrange("p u m e -> p u (m e)").bitcast(I32)
-                nc.vector.tensor_copy(
-                    out=page_bf[c][:].bitcast(I32).rearrange("p (m u) -> p m u", u=2),
-                    in_=words[:, :, half(c % 2)].rearrange("p u m -> p m u"),
-                )
-            if c > 0:
-                cols = half(c - 1)
-                nc.vector.quantize_mx(out=page_codes[:, cols].bitcast(FP8X4), scales=page_sc[:, cols], in_=page_bf[c - 1][:])
-                nc.sync.dma_start(out=words_out[:, cols], in_=page_codes[:, cols].bitcast(I32))
+        page_bf = [None] * CHUNKS
+
+        def weave_page(c):
+            page_bf[c] = shared([P, PACK * BANK], BF16, "page_bf%d" % c, ("w1_bf2", "w1_raw0", "tab1", "w1_raw0")[c])
+            words = pairs[c // 2][:].rearrange("p u m e -> p u (m e)").bitcast(I32)
+            nc.vector.tensor_copy(
+                out=page_bf[c][:].bitcast(I32).rearrange("p (m u) -> p m u", u=2),
+                in_=words[:, :, half(c % 2)].rearrange("p u m -> p m u"),
+            )
+
+        def quantise_page(c):
+            cols = half(c)
+            nc.vector.quantize_mx(out=page_codes[:, cols].bitcast(FP8X4), scales=page_sc[:, cols], in_=page_bf[c][:])
+            nc.sync.dma_start(out=words_out[:, cols], in_=page_codes[:, cols].bitcast(I32))
+
+        round_page(PACK - 1, BANK)
+        weave_x(0)
+        rate(0)
+        weave_x(1)
+        rate(1)
+        weave_page(0)
+        for c in range(CHUNKS):
+            if c + 1 < CHUNKS:
+                weave_page(c + 1)
+            quantise_page(c)
         for q in range(4):
             nc.scalar.dma_start(
                 out=out_3[0, 4 * q:4 * q + 4, :].bitcast(I32),

@@ -47,7 +47,7 @@ def tile_list_melt_pool_porosity_kernel(
 
         w2_sc_raw = keep.tile([P, PASSES, H], U8, name="w2_sc_raw", align_bytes=64)
         tab_sc = keep.tile([P, T], U8, name="tab_sc", align_bytes=64)
-        v_sc_low = keep.tile([P, PASSES - 1, S], U8, name="v_sc_low", align_bytes=64)
+        v_sc_low = shared([P, PASSES - 1, S], U8, "v_sc_low", "v_sc_low")
         nc.vector.memset(tab_sc[:].bitcast(I32), 0)
         nc.vector.memset(w2_sc_raw[:].rearrange("p a c -> p (a c)").bitcast(I32), 0)
         nc.vector.memset(v_sc_low[:].rearrange("p a c -> p (a c)").bitcast(I32), 0)
@@ -83,7 +83,7 @@ def tile_list_melt_pool_porosity_kernel(
         gs_sb = keep.tile([P, PACK], F32, name="gs_sb")
         nc.sync.dma_start(out=gs_sb[:], in_=gs.rearrange("(p t) -> p t", t=PACK))
 
-        w2_dealt = keep.tile([P, PASSES, 2 * H], U8, name="w2_dealt", align_bytes=64)
+        w2_dealt = shared([P, PASSES, 2 * H], U8, "w2_dealt", "w2_dealt")
         nc.vector.tensor_copy(
             out=w2_dealt[:].bitcast(U16).rearrange("p a (t m) -> p a t m", t=PACK),
             in_=w2_raw[:].bitcast(U16).rearrange("p a (m t) -> p a t m", t=PACK),
@@ -118,22 +118,13 @@ def tile_list_melt_pool_porosity_kernel(
         page = [keep.tile([P, T2], F32, name="page%d" % t) for t in range(PACK)]
         idx2 = lists.tile([P, S // 16], U16, name="idx2")
         idx3 = lists.tile([P, M_READ // 16], U16, name="idx3")
-        wg_first = keep.tile([P, S], F32, name="wg_first")
-        wg_rest = keep.tile([P, PACK - 1, S], F32, name="wg_rest")
         ginv_sb = keep.tile([P, PACK], F32, name="ginv_sb")
         w3_raw = keep.tile([P, PACK, N_OUT], F32, name="w3_raw")
         nc.sync.dma_start(out=page[0][:], in_=page_rows[0])
         nc.sync.dma_start(idx2[:], offs2)
-        for q in (0, 2, 1, 3):
-            nc.sync.dma_start(out=wg_first[QUAD * q:QUAD * (q + 1), :], in_=wgs_rows[:, 0, :])
         nc.sync.dma_start(idx3[:], offs3)
         nc.sync.dma_start(out=ginv_sb[:], in_=ginv.rearrange("(p t) -> p t", t=PACK))
         nc.sync.dma_start(out=page[1][:], in_=page_rows[1])
-        for q in (0, 2, 1, 3):
-            nc.sync.dma_start(out=wg_rest[QUAD * q:QUAD * (q + 1), :, :], in_=wgs_rows[:, 1:PACK, :])
-        nc.sync.dma_start(out=page[2][:], in_=page_rows[2])
-        nc.sync.dma_start(out=w3_raw[:], in_=w3.rearrange("(p j) n -> p j n", j=PACK))
-        nc.sync.dma_start(out=page[3][:], in_=page_rows[3])
 
         w1_codes = [keep.tile([P, H], U32, name="w1_codes%d" % a, align_bytes=64) for a in range(PASSES)]
         w1_sc = [keep.tile([P, H], U8, name="w1_sc%d" % a, align_bytes=64) for a in range(PASSES)]
@@ -150,8 +141,11 @@ def tile_list_melt_pool_porosity_kernel(
                 nc.vector.quantize_mx(
                     out=w1_codes[a][:, lo:hi].bitcast(FP8X4), scales=w1_sc[a][:, lo:hi], in_=w1_bf[:, PACK * lo:PACK * hi]
                 )
+        wg_first = shared([P, S], F32, "wg_first", "w1_raw1")
+        for q in (0, 2, 1, 3):
+            nc.scalar.dma_start(out=wg_first[QUAD * q:QUAD * (q + 1), :], in_=wgs_rows[:, 0, :])
 
-        sig = [keep.tile([P, S], F32, name="sig%d" % t) for t in range(PACK)]
+        sig = [shared([P, S], F32, "sig%d" % t, "sig%d" % t) for t in range(PACK)]
         hs = [None] * PACK
 
         def sigmoid_b(t):
@@ -174,7 +168,7 @@ def tile_list_melt_pool_porosity_kernel(
             hs[t] = shared([P, S], F32, "h%d" % t, "h")
             for n, lo in enumerate(range(0, S, width)):
                 cols = slice(lo, lo + width)
-                acc = psum.tile([P, width], F32, name="a_sum", tag="bank%d" % (2 + 2 * (t % 2) + n))
+                acc = psum.tile([P, width], F32, name="a_sum", tag="bank%d" % ((2 if t == 0 else 4) + n))
                 for a in range(PASSES):
                     nc.tensor.matmul_mx(
                         out=acc[:],
@@ -199,7 +193,6 @@ def tile_list_melt_pool_porosity_kernel(
             nc.sync.dma_start(out=out_rows[t], in_=page[t][:])
 
         cells = [shared([P, PACK, BANK], F32, "cells%d" % h, "tab%d" % h) for h in range(HALVES)]
-        gain = [shared([P, PACK, BANK], F32, "gain%d" % h, ("tab2", "w1_raw0")[h]) for h in range(HALVES)]
 
         def read_cells(t, width):
             pieces = [(lo // BANK, slice(lo % BANK, lo % BANK + width), slice(lo // 16, (lo + width) // 16))
@@ -235,12 +228,20 @@ def tile_list_melt_pool_porosity_kernel(
 
         sigmoid_b(0)
         make_h(0)
+        wg_rest = shared([P, PACK - 1, S], F32, "wg_rest", "sig0")
+        for q in range(4):
+            queue = nc.sync if q < 2 else nc.scalar
+            queue.dma_start(out=wg_rest[QUAD * q:QUAD * (q + 1), :, :], in_=wgs_rows[:, 1:PACK, :])
+        nc.sync.dma_start(out=page[2][:], in_=page_rows[2])
+        nc.sync.dma_start(out=w3_raw[:], in_=w3.rearrange("(p j) n -> p j n", j=PACK))
+        nc.sync.dma_start(out=page[3][:], in_=page_rows[3])
         sigmoid_b(1)
         scatter(0)
         pairs = [shared([P, 2, T2 // 2, 2], BF16, "pairs%d" % c, "w1_raw%d" % (c + 1)) for c in range(2)]
         sigmoid_b(2)
         make_h(1)
         sigmoid_b(3)
+        gain = [shared([P, PACK, BANK], F32, "gain%d" % h, ("w2_dealt", "v_sc_low")[h]) for h in range(HALVES)]
         for t in range(1, PACK):
             read_cells(t - 1, BANK)
             scatter(t)
@@ -287,7 +288,7 @@ def tile_list_melt_pool_porosity_kernel(
         page_bf = [None] * CHUNKS
 
         def weave_page(c):
-            page_bf[c] = shared([P, PACK * BANK], BF16, "page_bf%d" % c, ("w1_bf2", "w1_raw0", "tab1", "w1_raw0")[c])
+            page_bf[c] = shared([P, PACK * BANK], BF16, "page_bf%d" % c, ("w1_bf2", "v_sc_low", "tab1", "v_sc_low")[c])
             words = pairs[c // 2][:].rearrange("p u m e -> p u (m e)").bitcast(I32)
             nc.vector.tensor_copy(
                 out=page_bf[c][:].bitcast(I32).rearrange("p (m u) -> p m u", u=2),

from contextlib import ExitStack

import concourse.mybir as mybir

K, T, S, H, T2, M_READ, N_OUT = 1536, 2048, 1024, 512, 2048, 1024, 640
FLOPS = 2 * (2 * K * H * S + H * N_OUT * M_READ)

F32 = mybir.dt.float32
BF16 = mybir.dt.bfloat16
I32 = mybir.dt.int32
U32 = mybir.dt.uint32
U16 = mybir.dt.uint16
U8 = mybir.dt.uint8
FP8X4 = mybir.dt.float8_e4m3fn_x4
FP4X4 = mybir.dt.float4_e2m1fn_x4
ACT = mybir.ActivationFunctionType
ALU = mybir.AluOpType

P = 128
PACK = 4
PASSES = K // (P * PACK)
BANK = 512
HALVES = S // BANK
QUAD = 32
LIST_COLS = BANK // 16
CHUNKS = T2 // BANK


def tile_list_melt_pool_porosity_kernel(
    tc, tab_words, tab_scales, offs, offs2, offs3, w1, w2_words, w2_scales, gs, wgs, page0, ginv, w3,
    out_0, out_1, out_2, out_3,
):
    nc = tc.nc
    with ExitStack() as ctx:
        lists = ctx.enter_context(tc.tile_pool(name="lists", bufs=1))
        keep = ctx.enter_context(tc.tile_pool(name="keep", bufs=1))
        psum = ctx.enter_context(tc.psum_pool(name="psum", bufs=1))

        def shared(shape, dtype, name, tag):
            return keep.tile(shape, dtype, name=name, tag=tag, bufs=1, align_bytes=64)

        def half(h):
            return slice(h * BANK, (h + 1) * BANK)

        def list_half(tile, h):
            return tile[:, h * LIST_COLS:(h + 1) * LIST_COLS]

        w2_sc_raw = keep.tile([P, PASSES, H], U8, name="w2_sc_raw", align_bytes=64)
        tab_sc = keep.tile([P, T], U8, name="tab_sc", align_bytes=64)
        v_sc_low = shared([P, PASSES - 1, S], U8, "v_sc_low", "v_sc_low")
        nc.vector.memset(tab_sc[:].bitcast(I32), 0)
        nc.vector.memset(w2_sc_raw[:].rearrange("p a c -> p (a c)").bitcast(I32), 0)
        nc.vector.memset(v_sc_low[:].rearrange("p a c -> p (a c)").bitcast(I32), 0)
        for q in range(4):
            nc.scalar.dma_start(
                out=tab_sc[QUAD * q:QUAD * q + 4 * PASSES, :].bitcast(I32),
                in_=tab_scales[:, 4 * q:4 * q + 4, :].bitcast(I32),
            )
        for q in range(4):
            nc.scalar.dma_start(
                out=w2_sc_raw[QUAD * q:QUAD * q + 4, :, :].bitcast(I32),
                in_=w2_scales[:, 4 * q:4 * q + 4, :].rearrange("a r c -> r a c").bitcast(I32),
            )

        w2_raw = keep.tile([P, PASSES, 2 * H], U8, name="w2_raw", align_bytes=64)
        nc.sync.dma_start(out=w2_raw[:].bitcast(I32), in_=w2_words.rearrange("a p c -> p a c").bitcast(I32))
        idx = lists.tile([P, S // 16], U16, name="idx")
        nc.sync.dma_start(idx[:], offs)

        tab = [shared([P, T], I32, "tab%d" % a, "tab%d" % a) for a in range(PASSES)]
        w1_raw = [shared([P, PACK, H], F32, "w1_raw%d" % a, "w1_raw%d" % a) for a in range(PASSES)]

        def load_tab(a):
            nc.sync.dma_start(out=tab[a][:], in_=tab_words[a].rearrange("p t i -> p (t i)").bitcast(I32))

        def load_w1(a):
            rows = w1[a * P * PACK:(a + 1) * P * PACK, :]
            nc.sync.dma_start(out=w1_raw[a][:], in_=rows.rearrange("(p j) c -> p j c", j=PACK))

        for a in range(PASSES):
            load_tab(a)
            load_w1(a)
        gs_sb = keep.tile([P, PACK], F32, name="gs_sb")
        nc.sync.dma_start(out=gs_sb[:], in_=gs.rearrange("(p t) -> p t", t=PACK))

        w2_dealt = shared([P, PASSES, 2 * H], U8, "w2_dealt", "w2_dealt")
        nc.vector.tensor_copy(
            out=w2_dealt[:].bitcast(U16).rearrange("p a (t m) -> p a t m", t=PACK),
            in_=w2_raw[:].bitcast(U16).rearrange("p a (m t) -> p a t m", t=PACK),
        )
        v_words = [keep.tile([P, S], U32, name="v_words%d" % a, align_bytes=64) for a in range(PASSES)]
        v_sc = keep.tile([P, S], U8, name="v_sc", align_bytes=64)

        def gather_words(a):
            nc.vector.tensor_copy(v_words[a][:], tab[a][:].bitcast(U32).indirect(idx[:]))

        nc.vector.tensor_copy(v_sc[:], tab_sc[:].indirect(idx[:]))
        moved = 112
        for a in range(1, PASSES):
            nc.scalar.dma_start(
                out=v_sc_low[0:moved, a - 1, :].bitcast(I32),
                in_=v_sc[4 * a:4 * a + moved, :].bitcast(I32),
            )
        gather_words(0)
        w2_sc = keep.tile([P, PASSES, H], U8, name="w2_sc", align_bytes=64)
        nc.vector.tensor_copy(
            out=w2_sc[:].rearrange("p a (t m) -> p a t m", t=PACK),
            in_=w2_sc_raw[:].rearrange("p a (m t) -> p a t m", t=PACK),
        )
        gather_words(1)
        gather_words(2)
        neg_gs = keep.tile([P, PACK], F32, name="neg_gs")
        nc.vector.tensor_scalar(neg_gs[:], gs_sb[:], -1.0, None, ALU.mult)

        page_rows = page0.rearrange("(p t) c -> t p c", t=PACK)
        out_rows = out_1.rearrange("(p t) c -> t p c", t=PACK)
        wgs_rows = wgs.rearrange("(q t) j -> q t j", t=PACK)
        page = [keep.tile([P, T2], F32, name="page%d" % t) for t in range(PACK)]
        idx2 = lists.tile([P, S // 16], U16, name="idx2")
        idx3 = lists.tile([P, M_READ // 16], U16, name="idx3")
        ginv_sb = keep.tile([P, PACK], F32, name="ginv_sb")
        w3_raw = keep.tile([P, PACK, N_OUT], F32, name="w3_raw")
        nc.sync.dma_start(out=page[0][:], in_=page_rows[0])
        nc.sync.dma_start(idx2[:], offs2)
        nc.sync.dma_start(idx3[:], offs3)
        nc.sync.dma_start(out=ginv_sb[:], in_=ginv.rearrange("(p t) -> p t", t=PACK))
        nc.sync.dma_start(out=page[1][:], in_=page_rows[1])

        w1_codes = [keep.tile([P, H], U32, name="w1_codes%d" % a, align_bytes=64) for a in range(PASSES)]
        w1_sc = [keep.tile([P, H], U8, name="w1_sc%d" % a, align_bytes=64) for a in range(PASSES)]
        for a in range(PASSES):
            w1_bf = shared([P, PACK * H], BF16, "w1_bf%d" % a, "w1_bf%d" % a)
            dst = w1_bf[:].rearrange("p (t m j) -> p m j t", t=PACK, j=PACK)
            src = w1_raw[a][:].rearrange("p j (m t) -> p m j t", t=PACK)
            if a < PASSES - 1:
                nc.scalar.copy(out=dst, in_=src)
            else:
                nc.vector.tensor_copy(out=dst, in_=src)
            cuts = (0, H) if a < PASSES - 1 else (0, P, 2 * P, H)
            for lo, hi in zip(cuts, cuts[1:]):
                nc.vector.quantize_mx(
                    out=w1_codes[a][:, lo:hi].bitcast(FP8X4), scales=w1_sc[a][:, lo:hi], in_=w1_bf[:, PACK * lo:PACK * hi]
                )
        wg_first = shared([P, S], F32, "wg_first", "w1_raw1")
        for q in (0, 2, 1, 3):
            nc.scalar.dma_start(out=wg_first[QUAD * q:QUAD * (q + 1), :], in_=wgs_rows[:, 0, :])

        sig = [shared([P, S], F32, "sig%d" % t, "sig%d" % t) for t in range(PACK)]
        hs = [None] * PACK

        def sigmoid_b(t):
            for h in range(HALVES):
                acc = psum.tile([P, BANK], F32, name="b_sum", tag="bank%d" % (h if t == 0 else 2 + h))
                for a in range(PASSES):
                    v_plane = v_sc[:, half(h)] if a == 0 else v_sc_low[:, a - 1, half(h)]
                    nc.tensor.matmul_mx(
                        out=acc[:],
                        lhsT=w2_dealt[:, a, 2 * P * t:2 * P * (t + 1)].bitcast(FP4X4),
                        lhsT_scale=w2_sc[:, a, P * t:P * (t + 1)],
                        rhs=v_words[a][:, half(h)].bitcast(FP8X4),
                        rhs_scale=v_plane,
                        start=(a == 0), stop=(a == PASSES - 1),
                    )
                nc.scalar.activation(sig[t][:, half(h)], acc[:], ACT.Sigmoid)

        def make_h(t):
            width = BANK // 2 if t == 0 else BANK
            hs[t] = shared([P, S], F32, "h%d" % t, "h")
            for n, lo in enumerate(range(0, S, width)):
                cols = slice(lo, lo + width)
                acc = psum.tile([P, width], F32, name="a_sum", tag="bank%d" % ((2 if t == 0 else 4) + n))
                for a in range(PASSES):
                    nc.tensor.matmul_mx(
                        out=acc[:],
                        lhsT=w1_codes[a][:, P * t:P * (t + 1)].bitcast(FP8X4),
                        lhsT_scale=w1_sc[a][:, P * t:P * (t + 1)],
                        rhs=v_words[a][:, cols].bitcast(FP8X4),
                        rhs_scale=v_sc[4 * a:P, cols],
                        start=(a == 0), stop=(a == PASSES - 1),
                    )
                nc.vector.scalar_tensor_tensor(
                    hs[t][:, cols], sig[t][:, cols], neg_gs[:, t:t + 1], acc[:], ALU.mult, ALU.add
                )

        def scatter(t):
            if t == 0:
                for h in range(HALVES):
                    nc.vector.tensor_tensor(
                        page[t][:].indirect(list_half(idx2, h)), hs[t][:, half(h)], wg_first[:, half(h)], ALU.mult
                    )
            else:
                nc.vector.tensor_tensor(page[t][:].indirect(idx2[:]), hs[t][:], wg_rest[:, t - 1, :], ALU.mult)
            nc.sync.dma_start(out=out_rows[t], in_=page[t][:])

        cells = [shared([P, PACK, BANK], F32, "cells%d" % h, "tab%d" % h) for h in range(HALVES)]

        def read_cells(t, width):
            pieces = [(lo // BANK, slice(lo % BANK, lo % BANK + width), slice(lo // 16, (lo + width) // 16))
                      for lo in range(0, M_READ, width)]
            for h, cols, entries in pieces:
                nc.vector.tensor_copy(cells[h][:, t, cols], page[t][:].indirect(idx3[:, entries]))
            for first in range(0, len(pieces), 2):
                for h, cols, entries in pieces[first:first + 2]:
                    nc.scalar.activation(gain[h][:, t, cols], cells[h][:, t, cols], ACT.Abs, scale=ginv_sb[:, t:t + 1])
                for h, cols, entries in pieces[first:first + 2]:
                    nc.scalar.activation(gain[h][:, t, cols], gain[h][:, t, cols], ACT.Abs_reciprocal_sqrt, bias=1.0)
                for h, cols, entries in pieces[first:first + 2]:
                    nc.scalar.activation(gain[h][:, t, cols], gain[h][:, t, cols], ACT.Square)

        def round_page(t, width):
            for lo in range(0, T2, width):
                c, at = divmod(lo, T2 // 2)
                nc.scalar.copy(out=pairs[c][:, t // 2, at:at + width, t % 2], in_=page[t][:, lo:lo + width])

        w3_codes = keep.tile([P, N_OUT], U32, name="w3_codes", align_bytes=64)
        w3_sc = keep.tile([P, N_OUT], U8, name="w3_sc", align_bytes=64)

        def quantise_w3():
            w3_bf = shared([P, PACK * N_OUT], BF16, "w3_bf", "w1_bf0")
            nc.scalar.copy(
                out=w3_bf[:].rearrange("p (c i j) -> p c j i", i=4, j=PACK),
                in_=w3_raw[:].rearrange("p j (c i) -> p c j i", i=4),
            )
            for lo, hi in ((0, BANK), (BANK, N_OUT)):
                nc.vector.quantize_mx(
                    out=w3_codes[:, lo:hi].bitcast(FP8X4), scales=w3_sc[:, lo:hi], in_=w3_bf[:, PACK * lo:PACK * hi]
                )

        sigmoid_b(0)
        make_h(0)
        wg_rest = shared([P, PACK - 1, S], F32, "wg_rest", "sig0")
        for q in range(4):
            queue = nc.sync if q < 2 else nc.scalar
            queue.dma_start(out=wg_rest[QUAD * q:QUAD * (q + 1), :, :], in_=wgs_rows[:, 1:PACK, :])
        nc.sync.dma_start(out=page[2][:], in_=page_rows[2])
        nc.sync.dma_start(out=w3_raw[:], in_=w3.rearrange("(p j) n -> p j n", j=PACK))
        nc.sync.dma_start(out=page[3][:], in_=page_rows[3])
        sigmoid_b(1)
        scatter(0)
        pairs = [shared([P, 2, T2 // 2, 2], BF16, "pairs%d" % c, "w1_raw%d" % (c + 1)) for c in range(2)]
        sigmoid_b(2)
        make_h(1)
        sigmoid_b(3)
        gain = [shared([P, PACK, BANK], F32, "gain%d" % h, ("w2_dealt", "v_sc_low")[h]) for h in range(HALVES)]
        for t in range(1, PACK):
            read_cells(t - 1, BANK)
            scatter(t)
            round_page(t - 1, T2 // 2)
            if t + 1 < PACK:
                make_h(t + 1)
            if t == 2:
                quantise_w3()
        read_cells(PACK - 1, BANK // 2)

        x_codes = keep.tile([P, M_READ], U32, name="x_codes", align_bytes=64)
        x_sc = keep.tile([P, M_READ], U8, name="x_sc", align_bytes=64)
        x_bf = [None] * HALVES
        y_rows = out_0.rearrange("(b p) m -> b p m", p=P)

        def weave_x(h):
            x_bf[h] = shared([P, PACK * BANK], BF16, "x_bf%d" % h, "w1_bf1")
            nc.vector.tensor_tensor(
                x_bf[h][:].rearrange("p (c i t) -> p c t i", i=4, t=PACK),
                cells[h][:].rearrange("p t (c i) -> p c t i", i=4),
                gain[h][:].rearrange("p t (c i) -> p c t i", i=4),
                ALU.mult,
            )

        def rate(h):
            nc.vector.quantize_mx(out=x_codes[:, half(h)].bitcast(FP8X4), scales=x_sc[:, half(h)], in_=x_bf[h][:])
            for b in range(N_OUT // P):
                acc = psum.tile([P, BANK], F32, name="y_sum", tag="bank%d" % ((h * (N_OUT // P) + b) % 8))
                nc.tensor.matmul_mx(
                    out=acc[:],
                    lhsT=w3_codes[:, P * b:P * (b + 1)].bitcast(FP8X4),
                    lhsT_scale=w3_sc[:, P * b:P * (b + 1)],
                    rhs=x_codes[:, half(h)].bitcast(FP8X4),
                    rhs_scale=x_sc[:, half(h)],
                    start=True, stop=True,
                )
                y_sb = keep.tile([P, BANK], F32, name="y_sb", bufs=2 * (N_OUT // P))
                nc.scalar.copy(out=y_sb[:], in_=acc[:])
                nc.sync.dma_start(out=y_rows[b][:, half(h)], in_=y_sb[:])

        page_codes = keep.tile([P, T2], U32, name="page_codes", align_bytes=64)
        page_sc = keep.tile([P, T2], U8, name="page_sc", align_bytes=64)
        words_out = out_2[0].rearrange("p m t -> p (m t)").bitcast(I32)
        page_bf = [None] * CHUNKS

        def weave_page(c):
            page_bf[c] = shared([P, PACK * BANK], BF16, "page_bf%d" % c, ("w1_bf2", "v_sc_low", "tab1", "v_sc_low")[c])
            words = pairs[c // 2][:].rearrange("p u m e -> p u (m e)").bitcast(I32)
            nc.vector.tensor_copy(
                out=page_bf[c][:].bitcast(I32).rearrange("p (m u) -> p m u", u=2),
                in_=words[:, :, half(c % 2)].rearrange("p u m -> p m u"),
            )

        def quantise_page(c):
            cols = half(c)
            nc.vector.quantize_mx(out=page_codes[:, cols].bitcast(FP8X4), scales=page_sc[:, cols], in_=page_bf[c][:])
            nc.sync.dma_start(out=words_out[:, cols], in_=page_codes[:, cols].bitcast(I32))

        round_page(PACK - 1, BANK)
        weave_x(0)
        rate(0)
        weave_x(1)
        rate(1)
        weave_page(0)
        for c in range(CHUNKS):
            if c + 1 < CHUNKS:
                weave_page(c + 1)
            quantise_page(c)
        for q in range(4):
            nc.scalar.dma_start(
                out=out_3[0, 4 * q:4 * q + 4, :].bitcast(I32),
                in_=page_sc[QUAD * q:QUAD * q + 4, :].bitcast(I32),
            )
